import numpy as np, ml_dtypes
CORES = [3,11,19,27,35,43,51,59]
N = 8
BF = ml_dtypes.bfloat16
def gentries(a):
    return np.ascontiguousarray(a.reshape(8, 16, -1).transpose(0, 2, 1)).reshape(8, -1)
def gtable(e):
    e = np.asarray(e); return np.ascontiguousarray(e.reshape(8, -1, 16).transpose(0, 2, 1)).reshape(128, -1).astype(np.int32)
SO, RO, CR, CL, CF, TR = 384, 512, 256, 192, 64, 4
S, R = N * SO, N * RO
TH = 24
EPS = np.float32(0.125); UNDER = np.nextafter(EPS, np.float32(0)); LEAST = np.float32(0.00390625)
def expo(rng, lo, hi, *shape):
    return np.exp2(lo + (hi - lo) * rng.random(shape)).astype(np.float32)
def mark(rng, cnt):
    return np.argsort(rng.random((N, 8, 16, SO)), axis=2) < cnt[:, :, None, :]
def rows(rng, cnt):
    hi = np.maximum(expo(rng, -3, 0, N, 8, 16, SO), EPS); lo = np.minimum(expo(rng, -8, -3.1, N, 8, 16, SO), UNDER)
    return np.where(mark(rng, cnt), hi, lo)
def alive(cnt):
    return 2 * cnt + np.roll(cnt, -1, axis=1) >= TH
def lanes(rng, n):
    v = rng.random((N, 8, SO)); v[1::2, :, SO - 1] = -1.0
    return np.where(np.argsort(np.argsort(v, axis=2), axis=2) < n[:, :, None], 16, 0)
def react(rng, live, n):
    a = rng.integers(0, S, (N, 8, RO)); b = rng.integers(0, S, (N, 8, RO))
    for g in range(8):
        lv = np.flatnonzero(live[:, g]); dd = np.flatnonzero(~live[:, g])
        if lv.size == 0 or dd.size == 0: continue
        for q in range(N):
            v = rng.random(RO)
            if q % 2: v[RO - 1] = -1.0
            s = np.argsort(v)[:int(n[q, g])]; x = rng.choice(dd, (2, RO))
            x[0, s] = rng.choice(lv, len(s)); x[1, s] = rng.integers(0, S, len(s))
            x[1] = np.where(rng.random(RO) < 0.1, x[0], x[1]); sw = rng.random(RO) < 0.5
            a[q, g] = np.where(sw, x[1], x[0]); b[q, g] = np.where(sw, x[0], x[1])
    return a, b
def parts(rng):
    c = expo(rng, -0.5, 0.5, N, 8, 1, SO) * expo(rng, -0.25, 0.25, N, 8, 16, SO)
    share = rng.choice(np.array([0.3, 0.45, 0.6, 0.75]), (N, 8, 1))
    cnt = np.where(rng.random((N, 8, SO)) < share, rng.integers(9, 17, (N, 8, SO)), rng.integers(0, 8, (N, 8, SO)))
    e = rows(rng, cnt)
    goal = (rng.random((N, 8, 1, SO)) < 0.05) & (rng.random((N, 8, 16, SO)) < 0.75)
    tau = np.where(goal, np.float32(1), expo(rng, -8, -4, N, 8, 16, SO))
    hot = ((1.0 + 0.25 * rng.permutation(8)) * 0.0625).reshape(1, 8, 1, 1)
    k = np.where(rng.random((N, 8, 1, RO)) < hot, expo(rng, -0.75, 0.5, N, 8, 1, RO), expo(rng, -5, -3, N, 8, 1, RO)) * expo(rng, -0.5, 0.5, N, 8, 16, RO)
    return [c, e, tau, k, rng.integers(0, S, (N, 8, RO)), rng.integers(0, S, (N, 8, RO)), rng.integers(0, R, (N, 8, SO, 16)), rng.integers(0, S, (N, 8, SO, 16))]
def pack(c, e, tau, k, a, b, rx, ot):
    fl = lambda x, lo, hi: np.ascontiguousarray(np.clip(x.astype(np.float32), np.float32(lo), np.float32(hi)).reshape(N, 128, -1))
    ls = lambda x: np.stack([gtable(v.reshape(8, -1)) for v in x])
    return {"cin": fl(c, 0.125, 8), "ein": fl(e, 0.00390625, 1), "tau": fl(tau, 0.00390625, 1), "kin": fl(k, 0.015625, 2), "ra": ls(a), "rb": ls(b), "rx": ls(rx), "ot": ls(ot)}
def setup_inputs(rng):
    return pack(*parts(rng))
def setup_inputs_spread(rng):
    p = parts(rng)
    p[0] = np.clip(expo(rng, -3, 3, N, 8, 1, SO) * expo(rng, -0.5, 0.5, N, 8, 16, SO), 0.125, 8)
    p[3] = np.clip(expo(rng, -6, -1, N, 8, 1, RO) * expo(rng, -0.5, 0.5, N, 8, 16, RO), 0.015625, 2)
    return pack(*p)
def atend(rng, x, top, share):
    return np.where(rng.random(x.shape) < 0.72, np.where(rng.random(x.shape) < share, top, 0), x)
def setup_inputs_ends(rng):
    c, e, tau, k, a, b, rx, ot = parts(rng); q = N - 1
    n = rng.choice(np.array([CL // 2, CL - 1, CL, CL + 1, SO // 2, SO - CF]), (N, 8)); n[q] = CL - 1
    cnt = lanes(rng, n); mix = rng.random((N, 8, SO)) < 0.2; mix[q] = False
    cnt = np.where(mix, rng.choice(np.array([1, 7, 8, 11, 12, 15]), (N, 8, SO)), cnt)
    cnt[0, 7, :2] = 16; cnt[q, 7, SO - 2:] = 16
    e = np.where(mark(rng, cnt), np.float32(1), LEAST)
    ch = lambda w, share, hi, lo: rng.random((N, 8, 16, w)) < np.where(rng.random((N, 8, 1, w)) < share, hi, lo)
    c = np.where(ch(SO, 0.15, 0.9, 0.05), 8.0, 0.125); k = np.where(ch(RO, 0.25, 0.9, 0.08), 2.0, 0.015625); tau = np.where(ch(SO, 0.06, 0.9, 0.01), np.float32(1), LEAST)
    a = atend(rng, a, S - 1, 0.5); b = atend(rng, b, S - 1, 0.5); ot = atend(rng, ot, S - 1, 0.5)
    rx = atend(rng, rx, R - 1, np.where(rng.random((N, 8, SO, 1)) < 0.3, 0.5, 0.02))
    a[0, :, 0] = 0; b[0, :, 0] = 0; k[0, :, :, 0] = 0.015625; c[0, :, :, 0] = 0.125
    a[q, :, RO - 1] = S - 1; b[q, :, RO - 1] = S - 1; k[q, :, :, RO - 1] = 2.0; c[q, :, :, SO - 1] = 8.0
    rx[q, :, SO - 1, :8] = R - 1; rx[q, :, SO - 1, 8:] = 0; rx[q, :, SO - 2, :8] = 0; rx[q, :, SO - 2, 8:] = R - 1
    rx[0, :, 0, :8] = 0; rx[0, :, 0, 8:] = R - 1; rx[0, :, 1, :8] = R - 1; rx[0, :, 1, 8:] = 0
    c[q, 7, :, SO - 2] = 8.0; c[0, 7, :, 1] = 0.125
    a[q, :, RO - 17:RO - 1] = S - 1; b[q, :, RO - 17:RO - 1] = S - 1; k[q, :, :, RO - 17:RO - 1] = 2.0 - 0.03125 * rng.random((8, 16, 16))
    for g in range(8):
        h = rng.permutation(np.flatnonzero(cnt[q, g, :SO - 2] == 16))[:8]
        c[q, g][:, h] = 4.0; rx[q, g, h] = R - 17 + np.argsort(rng.random((len(h), 16)), axis=1)
    return pack(c, e, tau, k, a, b, rx, ot)
def setup_inputs_corners(rng):
    p = parts(rng); q = N - 1
    menu = np.array([0, 1, CL - 1, CL, CL + 1, SO, SO - CF, SO - CF + 1, SO - CF - 1, SO - 1, SO // 2]); n = rng.choice(menu, (N, 8))
    n[0] = menu[:8]; n[1] = rng.permutation(menu)[:8]; n[q] = np.where(np.arange(8) % 2 == 1, CL, SO - CF)
    m = np.array([0, 1, CR - 1, CR, CR + 1, RO, RO - 1, CR]); rn = rng.choice(m, (N, 8)); rn[0] = rng.permutation(m); rn[q] = m
    cnt = lanes(rng, n); p[1] = rows(rng, cnt); p[4], p[5] = react(rng, alive(cnt), rn)
    own = (np.arange(N)[:, None] * SO + np.arange(SO)[None, :])[:, None, :, None]
    z = rng.random((N, 8, SO, 16)); p[7] = np.where(z < 0.1, own, np.where(z < 0.15, 0, np.where(z < 0.2, S - 1, p[7])))
    z = rng.random((N, 8, SO, 16)); p[6] = np.where(z < 0.05, 0, np.where(z < 0.1, R - 1, p[6]))
    return pack(*p)
def setup_inputs_crowd(rng):
    c, e, tau, k, a, b, rx, ot = parts(rng)
    for g in range(8):
        x, y = int(rng.integers(0, S)), int(rng.integers(0, R))
        if g == 0: x, y = S - 1, R - 1
        if g == 1: x, y = 0, 0
        e[x // SO, g, :, x % SO] = 1.0 if g < 4 else LEAST; tau[x // SO, g, :, x % SO] = 1.0 if g < 4 else LEAST
        if g % 4 == 0: a[:, g] = x; b[:, g] = x; rx[:, g] = y; ot[:, g] = x
        if g % 4 == 1:
            j = int(rng.integers(0, RO)); a[:, g, :j] = x; a[:, g, j + 1:] = x; b[:, g, :j] = x; b[:, g, j + 1:] = x
            rx[:, g, :, :15] = y; ot[:, g, :, :15] = x
        if g % 4 == 2:
            sp = np.array([x, (x + 1) % S, (x + SO) % S]); rc = np.array([y, (y + 1) % R, (y + RO) % R])
            a[:, g] = rng.choice(sp, (N, RO)); b[:, g] = rng.choice(sp, (N, RO)); rx[:, g] = rng.choice(rc, (N, SO, 16)); ot[:, g] = rng.choice(sp, (N, SO, 16))
        if g % 4 == 3: a[:, g] = x; rx[:, g, :, :8] = y
    return pack(c, e, tau, k, a, b, rx, ot)
def setup_inputs_calm(rng):
    p = parts(rng); i = 3 * np.arange(N)[:, None] + np.arange(8)[None, :]; q = N - 1
    n = np.array([0, 1, 2, 3, SO - 1, SO, CL, CL + 1])[i % 8]; n[1, 4:] = CL
    cnt = lanes(rng, n); keep = np.array(cnt[1, 4:])
    cnt[1::2] = rng.choice(np.array([0, 1, 2, 7, 8, 11, 12, 15, 16]), cnt[1::2].shape)
    v = rng.permutation(SO // 4); z, u = int(v[0]), int(v[1]); chain = v[2:7]; lapse = v[7:15]; rise = v[15:23]
    gg = SO // 4 + rng.permutation(CL - SO // 4)[:8]
    cnt[1, 4:] = keep; cnt[1, :2] = 16; cnt[1][:2, chain] = 0; cnt[1, 2] = 0; cnt[1, 3] = 16
    cnt[q][:, gg] = 16; cnt[q][:, z] = 16; cnt[q][:, u] = 0
    half = rng.random((N, 8, 16, SO)) < 0.5
    p[2] = np.where(mark(rng, cnt), np.where(half, EPS, np.float32(1)), np.where(half, UNDER, expo(rng, -8, -6, N, 8, 16, SO))); p[1] = np.array(p[2])
    p[0] = expo(rng, -1, 0.5, N, 8, 1, SO) * expo(rng, -0.25, 0.25, N, 8, 16, SO); p[3] = expo(rng, -6, -5.5, N, 8, 16, RO)
    lv = alive(cnt); p[4], p[5] = react(rng, lv, np.array([0, 1, 2, 3, RO - 1, RO, CR - 1, CR])[(i + 2) % 8])
    c, e, tau, k, a, b, rx, ot = p
    for x in (a, b):
        x[:, 2] = np.where(np.isin(x[:, 2], SO + lapse), q * SO + u, x[:, 2]); x[:, 3] = np.where(np.isin(x[:, 3], SO + rise), q * SO + z, x[:, 3])
        x[1, 2] = SO + rng.choice(lapse, RO)
    e[1, 2][:, lapse] = 1.0; tau[1, 2][:, lapse] = LEAST
    e[1, 3][:, rise] = LEAST
    for g in range(8):
        d = 2.0 ** -int(rng.integers(13, 20)); y, y2 = [int(x) for x in rng.permutation(RO)[:2]]; s = int(rng.integers(0, 16))
        flat = lv[:, g].reshape(-1)
        for j, rate in ((y, 0.5 * (1.0 - d)), (y2, 0.875)):
            x = q * SO + (z if flat[a[q, g, j]] or flat[b[q, g, j]] else u)
            a[q, g, j] = x; b[q, g, j] = x; k[q, g, :, j] = rate
        rx[:, g] = np.where((rx[:, g] == q * RO + y) | (rx[:, g] == q * RO + y2), rx[:, g] - q * RO, rx[:, g])
        c[q, g][:, [z, u]] = 1.0; rx[q, g, z, 8:] = rx[q, g, z, :8]
        e[q, g, :, z] = 0.25 * (1.0 + d); tau[q, g, :, z] = 0.25 * (1.0 + d)
        tau[q, g][:, gg] = LEAST; e[q, g][:, gg] = EPS; rx[q, g, gg, s] = q * RO + y; ot[q, g, gg, s] = q * SO + z
        if g < 2:
            src = q * SO + int(gg[0])
            for x in chain:
                e[1, g, :, x] = LEAST; tau[1, g, :, x] = LEAST; rx[1, g, x] = q * RO + y2; ot[1, g, x] = src; src = SO + int(x)
        if g >= 4:
            ot[1, g] = q * SO + rng.integers(0, SO, (SO, 16)); ot[1, g, SO - 1, 15] = q * SO + z; rx[1, g, SO - 1, 15] = q * RO + y
            tau[1, g, :, SO - 1] = LEAST; e[1, g, :, SO - 1] = EPS; c[1, g, :, SO - 1] = 1.0
    return pack(c, e, tau, k, a, b, rx, ot)
def check_inputs(d):
    bad = []
    for k, lo, hi in (("cin", 0.125, 8), ("ein", 0.00390625, 1), ("tau", 0.00390625, 1), ("kin", 0.015625, 2), ("ra", 0, S - 1), ("rb", 0, S - 1), ("rx", 0, R - 1), ("ot", 0, S - 1)):
        if not (np.min(d[k]) >= lo and np.max(d[k]) <= hi): bad.append("range of " + k)
    return bad
def first(flag, start, cap):
    f = np.roll(flag, -start, axis=2).astype(np.int64); before = np.add.accumulate(f, axis=2) - f
    return np.roll((f == 1) & (before < cap), start, axis=2)
def reference(cin, ein, tau, kin, ra, rb, rx, ot):
    F = np.float32
    glue = lambda x: np.array(x.astype(F).reshape(N, 8, 16, -1).transpose(1, 2, 0, 3), order="C").reshape(8, 16, -1)
    lst = lambda x: np.stack([gentries(v) for v in x]).astype(np.int64).transpose(1, 0, 2).reshape(8, -1)
    C, E, low, k = glue(cin), glue(ein), glue(tau), glue(kin)
    A, B = lst(ra), lst(rb); RX, OT = lst(rx).reshape(8, S, 16), lst(ot).reshape(8, S, 16)
    w = np.stack([(k[g] * C[g][:, A[g]]) * C[g][:, B[g]] for g in range(8)])
    for t in range(TR):
        cnt = np.add.reduce((E >= EPS).astype(np.int64), axis=1)
        live = 2 * cnt + np.roll(cnt, -1, axis=0) >= TH
        act = np.take_along_axis(live, A, 1) | np.take_along_axis(live, B, 1)
        mr = first(act.reshape(8, N, RO), (t * (RO // 4)) % RO, CR).reshape(8, R)
        ml = first(live.reshape(8, N, SO), (t * (SO // 4)) % SO, CL).reshape(8, S)
        mf = first(~live.reshape(8, N, SO), (t * (SO // 4)) % SO, CF).reshape(8, S)
        for g in range(8):
            j = np.flatnonzero(mr[g]); w[g][:, j] = (k[g][:, j] * C[g][:, A[g, j]]) * C[g][:, B[g, j]]
        for sweep in range(2):
            for g in range(8):
                s = np.flatnonzero(ml[g] | mf[g])
                p = E[g][:, OT[g, s].reshape(-1)] * np.minimum(w[g][:, RX[g, s].reshape(-1)], F(1))
                E[g][:, s] = np.maximum(low[g][:, s], np.max(p.reshape(16, len(s), 16), axis=2))
        for g in range(8):
            s = np.flatnonzero(ml[g]); x = w[g][:, RX[g, s].reshape(-1)].reshape(16, len(s), 16)
            for level in range(3): x = x[:, :, 0::2] + x[:, :, 1::2]
            C[g][:, s] = np.minimum(np.maximum(C[g][:, s] + (x[:, :, 0] - x[:, :, 1]) * F(0.125), F(0.125)), F(8))
    back = lambda x: np.ascontiguousarray(x.reshape(8, 16, N, -1).transpose(2, 0, 1, 3)).reshape(N, 128, -1)
    return {"yc": back(C), "ye": back(E), "yw": back(w)}

import numpy as np
from concourse.bass import DstId, RemoteDMATransfer
from concourse.mybir import AluOpType as ALU, ActivationFunctionType as ACT

N = 8
SO, RO, TR = 384, 512, 4
F32, BF, I32, U16 = "float32", "bfloat16", "int32", "uint16"

NDIRECT = ("WPEP", "EPPP")
W_PE = 4
W8_PE = 0
GG_S = 1
C_PE = 4
C0_PE = 4
E0_PE = 5
HEAD_PE = (0, 0)
TAIL_PE = (7, 3)
SEED, PASSES, NOISE, VCOST = 0, 4, 0.5, 0.0
PLAN = {}
ENGINE, BIAS = {}, {}
SHIFT, PERIOD = {}, 44.0
C_SPLIT = False

_SB = {
    F32: dict(TE=3456, CT=3072, WM=4096, W8=4096, WC=2048, KK=512, T1=512, YW=512, EG=4096, MW=4096, RW=4096, PR=4096,
              SC=4104, MK=1024, T2=384, CX=384, DD=264, YE=2048, ZE=1024, PP=512, A1=64, A2=64, CN=96, NB=96, TH=24, KC=48,
              YY=48, OO=48, PL=48, PS1=24, PKD=24, TT=24, TL=24, SF=24, Q1=24, Q2=24, JT=128, V384=24, FJ=32, M2=32, O2=32,
              OF=32, XI=256, PC=8, I2=256, K16=16, U1=128, U2=128),
    I32: dict(RXI=384, OTI=384, OT2=384, PKS=384, PK=384, CP=648, LI=256, AB=64, A3=64, A4=64, A5=64, PCI=8),
    U16: dict(LRA=384, LOA=384, LR=256, LO=256, OA=64, CA=64, AM=64, SCO=24, BK=24, BC=24, TQ=24, OW=32),
    BF: dict(FL=384, LF=48, F1=24, FF=48, L2=192, MA=1024, GG=1024, GB=1024, G1=32, G2=32, ZZ=144, IB=256, BD=128, NBD=128, NU=128),
}
SCRATCH = {}
for _dt in _SB:
    for _n in _SB[_dt]:
        SCRATCH[_n] = ("sbuf", [128, _SB[_dt][_n]], _dt)
for _n, _w, _dt in (("CD", 48, F32), ("ED", 48, F32), ("ABD", 8, I32), ("KD", 64, F32), ("PD", 48, I32), ("TD", 48, F32),
                    ("OC", 48, F32), ("OE", 24, F32), ("OH", 24, F32), ("OWD", 64, F32)):
    SCRATCH["s" + _n] = ("dram", [N, 128, _w], _dt)
    SCRATCH["r" + _n] = ("dram", [N, 128, _w], _dt)
SCRATCH["PS"] = ("psum", [128, 4096], F32)

NDMA = 100
SEMAPHORES = ["qV", "qS", "qP", "qG", "left"] + ["d%d" % i for i in range(NDMA)] + ["a%d" % i for i in range(16)]

PACE = [(1.04e-3, 0.52e-3, 1.56, 1.8, 3.8, 0.08, 2.0, 2.5, 0.045, 25e3, 0.6),
        (1.15e-3, 0.58e-3, 1.95, 2.0, 5.0, 0.12, 2.3, 3.2, 0.065, 19e3, 0.3)]
HOP = PACE[0][5]
DIGITS = "0123456789abcdefghijklmnopqrstuvwxyzABCDEFGHIJKLMNOPQRSTUVWXYZ"
ORDER = "0002160a0i180m1c0u101g0g1e0C2a1i081k1y1w0k1A0A1m20261C041Y0Y1M281W0s0K1q0M1s1G060o0O0c0q0E0G0I2c0Q0e1a0w0S2g1o1E1u221K241I2w2e1O1U1Q1S0y2o2i0U2s2r2k2v2W2z2G2A2Y2I0W3e302K322M2S3i2U2m3z12342O363a2Q2C3u3m3d383h3q143w3l3p3G3I3K4q4K3M4y4B3t4s4C4u3O3Q3A3S3U3W3Y40424i4c443E463C484k4a4O4m4G4F4x4J2E4M4R4Y5e4W4p4T505a5g5m5o5i5c5k5u5w5q5y5266544U5A5s5C5E5M5I685G6a5U6c5O5K5Q5Y624e4g5W5T61656e6g6i6k6m6E6M6C6s6K6u586y6o6A6q6G6O6I6Q6w6Y7E707G6S72567y746W767A7C787I7K6U7u7a7q7x7M7c7O7Q7m7t7e7g7S7U7W8c88807p8f7Y7i8k8b8E8m8G8o8I8r8y82848w7k8K8M8s8A8Q878u8C8g9o8O9q9u9s8i9w9y8S9A9C9E8U9G8Wa5a09I8Y909W9S9O9K9294969Z989g9i9Q9k9a9Va79Na29maqauacaea9awagayasaCaAaEaKaMaGaOaiakbCaQaIaSaUbEbGb2beb8aWb4b69cbIbqbabgaY9ebcbib0bKbMbwbkbsaabzbBbvbnbpbObQcac8cibSbUc4bYc0cgccc6ckcec2amcucwcycmcAdecocCcEbWdgcIcscGaodkdidmcKcqd8d2dbdddocMdqdscOcWd5d7cQdudwdydAdCdEdOdGcYd0cSe2e0ekeme4eodRe7dIdSecdKeqewe8eeeseueyegdVdNcUeaeidWf4f6faf8fcdYfefgfifkfmeSfGfufCfyfqfLeWeYeAf0f3fFeCfoeEeGeQeIeKeMfweOfNfIfAfsgafUg6gcfSgifPgeg8gkggfWgsgqfYgmgug0h2gwgogyh4h6gIgAgEh8gCeUgGgMgQgLgYfQhahcgTgPgUh1gXhAhehghihkhohyhIg2hqhshmhuhGhChEhwiuhWhUiwhKhMhYhOi0g4iAi2hSi4iyiChQi6iEi8iGiIiqiKiMiOiiimiaitiQiSipj8iWiciUikiejgjkjniZjujijAjCjEj0jsj4jaj3jGjIjojKjOkcjwj7jcigjqjykkkmkqkoksjekukwkykAkCjMldkekgkSl1kjkVkWkOkKjQkRjSjUjWjYk0k2lfkEkGk8k4kYkMk6kIlClmlylElKlklGlMlAlIlhlomcmel2l4lqmglOlQmOlUlsmQmSm0mUlXmililulYmkmWm2m6m4mqmmmul6lSl8msm8mamymomCmwmKmGmYn0n2kan4n6mMn8lamFmBmJngnknmnsnanoninunco8nwoanqnyoclwoeogneoinAokomoooqnCosnQnOounEownSnUnWoynGnIoCoAnYoEnKnMo0o2oGo4o6"


def build(g, core, T, topo, pace):
    CYC, PEC, GAT, GTT, SCA, _, DLAT, RLAT, DROW, DBW, _ = pace
    rank = T.rank_of(core)
    ops, hist, cnt = [], {}, {"d": 0, "a": 0, "left": 0, "bank": 0}
    part = ["i", 0]
    Q = {"V": g.vector, "S": g.scalar, "P": g.tensor, "G": g, "Y": g.sync}

    def sb(name, c0=0, c1=None, step=1, p0=0, p1=128):
        if c1 is None:
            c1 = T[name].shape[1]
        ap = T[name][p0:p1, c0:c1:step] if step > 1 else T[name][p0:p1, c0:c1]
        return {"ap": ap, "r": [(name, p0, p1, c0, c1)], "n": len(range(c0, c1, step)), "ps": name == "PS", "ind": False}

    def ps(bank, c0, c1, step=1):
        return sb("PS", 512 * bank + c0, 512 * bank + c1, step)

    def dr(name, s0, s1, r0=0, r1=128):
        return {"ap": T[name][s0:s1, r0:r1, :], "r": [(name, s0, s1, r0, r1)]}

    def io_(name, p0=0, p1=128):
        return {"ap": T[name][p0:p1, :], "r": []}

    def ind(win, off):
        return {"ap": win["ap"].indirect(off["ap"]), "r": win["r"], "o": off["r"], "n": 16 * off["n"], "ps": False, "ind": True}

    def op(eng, fn, reads, writes, dur, lat=0.0, kind="c", after=()):
        me, deps = len(ops), {}
        rr, ww = [], []
        for a in reads:
            rr += a["r"] + a.get("o", [])
        for a in writes:
            ww += a["r"]
            rr += a.get("o", [])
        for regs, isw in ((rr, False), (ww, True)):
            for (nm, p0, p1, c0, c1) in regs:
                for (o, ow, q0, q1, d0, d1) in hist.get(nm, []):
                    if (ow or isw) and p0 < q1 and q0 < p1 and c0 < d1 and d0 < c1:
                        deps[o] = "data"
                    elif nm == "PS" and c0 // 512 <= (d1 - 1) // 512 and d0 // 512 <= (c1 - 1) // 512:
                        deps.setdefault(o, "bank")
        for regs, isw in ((rr, False), (ww, True)):
            for (nm, p0, p1, c0, c1) in regs:
                h = hist.setdefault(nm, [])
                if isw:
                    h[:] = [e for e in h if not (p0 <= e[2] and e[3] <= p1 and c0 <= e[4] and e[5] <= c1)]
                h.append((me, isw, p0, p1, c0, c1))
        for o in after:
            deps[o] = "order"
        if not isinstance(dur, dict):
            dur = {e: dur for e in eng}
        named = [r for r in ww if r[0] != "PS"] or [r for r in reversed(rr) if r[0] != "PS"] or [("y", 0, 0, 0, 0)]
        tag = part[0] + (eng if len(eng) == 1 else "F") + named[0][0] + (str(named[0][3] // 1024) if named[0][0] in ("EG", "MW", "RW", "PR", "SC") else "")
        if len(eng) > 1:
            eng = ENGINE.get(tag, eng)
        ops.append({"eng": eng, "fn": fn, "deps": deps, "dur": dur, "lat": lat, "kind": kind, "tag": tag, "round": part[1]})
        return me

    def vt(n):
        return max(64.0, n) * CYC + 0.05

    def sc_(x):
        return x["ap"] if isinstance(x, dict) else x

    def tt(out, a, b, alu):
        n = out["n"] * (GTT if a["ind"] else (1 if a["ps"] or b["ps"] else 2))
        return op("V", lambda e: [g.vector.tensor_tensor(out["ap"], a["ap"], b["ap"], alu)], [a, b], [out], vt(n))

    def ts(out, a, s1, o1, s2=None, o2=None):
        rd = [a] + [s for s in (s1, s2) if isinstance(s, dict)]
        if o2 is None:
            fn = lambda e: [g.vector.tensor_scalar(out["ap"], a["ap"], sc_(s1), None, o1)]
        else:
            fn = lambda e: [g.vector.tensor_scalar(out["ap"], a["ap"], sc_(s1), sc_(s2), o1, o2)]
        return op("V", fn, rd, [out], vt(out["n"] * (GAT if a["ind"] else 1)))

    def cp(out, a, eng="V", scale=None):
        def fn(e):
            if e == "V":
                return [g.vector.tensor_copy(out["ap"], a["ap"])]
            if scale is None:
                return [g.scalar.activation(out["ap"], a["ap"], ACT.Copy)]
            return [g.scalar.activation(out["ap"], a["ap"], ACT.Copy, scale=scale)]
        n = a["n"] * (SCA if out["ind"] else (GAT if a["ind"] else 1))
        return op(eng, fn, [a], [out], {"V": vt(n), "S": vt(n) + 0.03})

    def scan(out, d0, d1, init, o0, o1):
        rd = [d0, d1] + ([init] if isinstance(init, dict) else [])
        return op("V", lambda e: [g.vector.tensor_tensor_scan(out["ap"], d0["ap"], d1["ap"], sc_(init), o0, o1)], rd, [out], vt(out["n"]))

    def fill(out, v):
        return op("V", lambda e: [g.vector.memset(out["ap"], v)], [], [out], vt(out["n"]))

    def mm(items, wide):
        fn = lambda e: [g.tensor.matmul(o["ap"], l["ap"], r["ap"], a, b) for (o, l, r, a, b) in items]
        dur = sum(max(64, r["n"]) * (4 if wide else 1) * PEC for (o, l, r, a, b) in items) + 0.03
        return op("P", fn, [x[1] for x in items] + [x[2] for x in items], [x[0] for x in items], dur, lat=0.1)

    def dma(pairs, rows, rowbytes, eng="Y", nom=0):
        t = max(rows * (DROW + rowbytes / DBW) / 16, 0.06 * (nom or len(pairs)))
        fn = lambda e: [Q[e].dma_start(o["ap"], i["ap"]) for (o, i) in pairs]
        if eng == "Y":
            me = op(eng, fn, [p[1] for p in pairs], [p[0] for p in pairs], t, lat=DLAT, kind="d")
        else:
            me = op(eng, fn, [p[1] for p in pairs], [p[0] for p in pairs], 0.06 * len(pairs), lat=DLAT + t, kind="d")
        ops[me]["sem"] = "d%d" % cnt["d"]
        cnt["d"] += 1
        return me

    def bank():
        cnt["bank"] += 1
        if part[0] == "h":
            return 2 + cnt["bank"] % 2
        return 3 + cnt["bank"] % 3 if part[0] in "uj" else 2 + cnt["bank"] % 4

    def plan(src):
        dsts = [c for c in T.cores if c != src]
        free = [e for e in topo.engines(src, dsts[0]) if all(e in topo.engines(src, c) for c in dsts)]
        got = {c: [free[i]] for i, c in enumerate(dsts)}
        far = [c for c in dsts if not topo.mates(topo.chip(src), topo.chip(c)) and not topo.same_plane(topo.chip(src), topo.chip(c))]
        for e, c in zip(free[len(dsts):], far):
            got[c].append(e)
        return got

    def all_to_all(name, kb):
        sem = "a%d" % cnt["a"]
        cnt["a"] += 1
        mine = plan(core)

        def fn(e):
            tr = []
            for c in mine:
                rid, pid, _ = topo.addr(c)
                tr.append(RemoteDMATransfer(dst_ids=[DstId(rid=rid, pnc=pid)], dma_engine_mask=sum(1 << x for x in mine[c]),
                                            remote_sem=T.sem[sem], src=T["s" + name][T.rank_of(c)], dst=T["r" + name][rank]))
            g.remote_dma_fused(tr, local_sem=T.sem.left)
            return []
        cnt["left"] += sum(len(v) for v in mine.values())
        s = op("G", fn, [dr("s" + name, 0, N)], [], 0.5 + kb / 14.0, kind="r")
        land = [dr("r" + name, q, q + 1) for q in range(N) if q != rank]
        me = op("R", None, [], land, 0.0, lat=RLAT, kind="a", after=[s])
        ops[me]["tok"] = (sem, sum(len(plan(c)[core]) for c in T.cores if c != core))

    def widest(src, dst):
        es = topo.engines(src, dst)
        k = 1
        while 2 * k <= len(es):
            k *= 2
        return es[:k]

    def pass_counts(t):
        sem = "a%d" % cnt["a"]
        cnt["a"] += 1
        dst, src = T.cores[(rank - 1) % N], T.cores[(rank + 1) % N]
        es = widest(core, dst)
        a, b = sb("CN", 24 * t, 24 * t + 24), sb("NB", 24 * t, 24 * t + 24)

        def fn(e):
            rid, pid, _ = topo.addr(dst)
            g.remote_dma(b["ap"], a["ap"], T.sem[sem], T.sem.left, pid, rid, sum(1 << x for x in es))
            return []
        cnt["left"] += len(es)
        s = op("G", fn, [a], [], 0.8, kind="r")
        me = op("R", None, [], [b], 0.0, lat=RLAT + 0.5, kind="a", after=[s])
        ops[me]["tok"] = (sem, len(widest(src, core)))

    def spread(name, base, width, ranges, npe, evac="VS"):
        byd = list(range(1, N - npe))
        if byd:
            pairs = []
            for d in byd:
                for (c0, c1) in ranges:
                    o = base + width * d
                    pairs.append((sb(name, o + c0, o + c1, p0=0, p1=128 - 16 * d), sb(name, base + c0, base + c1, p0=16 * d, p1=128)))
                    pairs.append((sb(name, o + c0, o + c1, p0=128 - 16 * d, p1=128), sb(name, base + c0, base + c1, p0=0, p1=16 * d)))
            dma(pairs, 128 * len(byd) * len(ranges), 4 * (ranges[0][1] - ranges[0][0]))
        for d in range(N - npe, N):
            b, at, items = bank(), 0, []
            for (c0, c1) in ranges:
                items.append((ps(b, at, at + c1 - c0), sb("I2", 16 * d, 16 * d + 128), sb(name, base + c0, base + c1), True, True))
                at += c1 - c0
            mm(items, True)
            at = 0
            for (c0, c1) in ranges:
                cp(sb(name, base + width * d + c0, base + width * d + c1), ps(b, at, at + c1 - c0), evac)
                at += c1 - c0

    def load_slots(name, base, src, slots):
        pairs = []
        for d in slots:
            o = base + SO * d
            pairs.append((sb(name, o, o + SO, p0=0, p1=128 - 16 * d), dr(src, d, N)))
            if d:
                pairs.append((sb(name, o, o + SO, p0=128 - 16 * d, p1=128), dr(src, 0, d)))
        dma(pairs, 128 * len(slots), 4 * SO)

    def go_home(name, nm, base, ranges, y):
        rows, wd = 128 // len(ranges), ranges[0][1] - ranges[0][0]
        kb = wd * len(ranges) / 16.0
        yy = lambda p0, p1, c0, c1: {"ap": T[y][p0:p1, c0:c1], "r": []}
        dma([(dr("s" + name, 0, N, rows * j, rows * j + rows), sb(nm, base + c0, base + c1)) for j, (c0, c1) in enumerate(ranges)],
            128 * len(ranges), 4 * wd)
        dma([(yy(16 * rank, 16 * rank + 16, c0, c1), sb(nm, base + c0, base + c1, p0=16 * rank, p1=16 * rank + 16)) for (c0, c1) in ranges],
            16 * len(ranges), 4 * wd)
        all_to_all(name, kb)
        pairs = [(yy(16 * a, 16 * b, c0, c1), dr("r" + name, a, b, rows * j, rows * j + rows))
                 for j, (c0, c1) in enumerate(ranges) for (a, b) in ((0, rank), (rank + 1, N)) if a < b]
        dma(pairs, 112 * len(ranges), 4 * wd, nom=2 * len(ranges))

    def rot(n, p):
        return [(p, n), (0, p)] if p else [(0, n)]

    def count_up(out, flag, n, p, init):
        last = init
        for (c0, c1) in rot(n, p):
            scan(sb(out, c0, c1), sb(flag, c0, c1), sb(flag, c0, c1), last, ALU.add, ALU.max)
            last = sb(out, c1 - 1, c1)

    ETAB = sb("TE", SO, SO + N * SO)
    own = slice(16 * rank, 16 * rank + 16)

    def stage(name, x, r0, r1, kb):
        dma([(dr("s" + name, 0, N, r0, r1), io_(x))], 16, kb * 512)
        dma([(dr("r" + name, rank, rank + 1, r0, r1), io_(x, own.start, own.stop))], 16, kb * 64, "S")
    stage("CD", "cin", 0, 128, 24)
    all_to_all("CD", 24)
    stage("ED", "ein", 0, 128, 24)
    all_to_all("ED", 24)
    stage("ABD", "ra", 0, 64, 2)
    stage("ABD", "rb", 64, 128, 2)
    all_to_all("ABD", 4)
    stage("KD", "kin", 0, 128, 32)
    all_to_all("KD", 32)
    dma([(sb("RXI"), io_("rx"))], 128, 4 * SO)
    dma([(sb("OTI"), io_("ot"))], 128, 4 * SO)
    ts(sb("RXI"), sb("RXI"), N * RO - RO * rank, ALU.add)
    ts(sb("RXI"), sb("RXI"), N * RO - 1, ALU.bitwise_and)
    ts(sb("RXI"), sb("RXI"), float(N * RO), ALU.mult)
    ts(sb("OT2"), sb("OTI"), SO * rank, ALU.is_lt, N * SO, ALU.mult)
    ts(sb("OTI"), sb("OTI"), SO * rank, ALU.subtract)
    tt(sb("OTI"), sb("OTI"), sb("OT2"), ALU.add)
    tt(sb("PKS"), sb("RXI"), sb("OTI"), ALU.add)
    dma([(dr("sPD", 0, N), sb("PKS")), (dr("rPD", rank, rank + 1), sb("PKS", p0=own.start, p1=own.stop))], 128, 4 * SO)
    all_to_all("PD", 24)
    stage("TD", "tau", 0, 128, 24)
    all_to_all("TD", 24)

    def iota(out, pattern, base, cm, flag):
        if flag:
            fn = lambda e: [g.iota(out["ap"], pattern, base, cm, allow_small_or_imprecise_dtypes=True)]
        else:
            fn = lambda e: [g.iota(out["ap"], pattern, base, cm)]
        op("G", fn, [], [out], 0.15 + 2 * out["n"] * CYC)
    iota(sb("PCI", 0, 1), [[0, 1]], 0, 1, False)
    iota(sb("XI"), [[1, 256]], 0, 0, True)
    iota(sb("FF"), [[0, 2], [1, 24]], 25, 0, True)
    col = lambda k: sb("PC", k, k + 1)
    ts(sb("PCI", 1, 2), sb("PCI", 0, 1), 15, ALU.bitwise_and)
    cp(col(0), sb("PCI", 0, 1))
    cp(col(1), sb("PCI", 1, 2))
    tt(col(2), col(0), col(1), ALU.subtract)
    ts(col(3), col(2), 15.0, ALU.add)
    ts(col(4), col(2), SO / 16.0, ALU.mult)
    for nm in ("I2", "IB"):
        for h in (0, 128):
            ts(sb(nm, h, h + 128), sb("XI", 0, 128), col(0), ALU.is_equal)
    ts(sb("ZZ"), sb("XI", 0, 144), col(3), ALU.is_equal)
    ts(sb("U1"), sb("XI", 0, 128), col(2), ALU.is_ge)
    ts(sb("U2"), sb("XI", 0, 128), col(3), ALU.is_le)
    tt(sb("BD"), sb("U1"), sb("U2"), ALU.mult)
    ts(sb("NBD"), sb("BD"), -1.0, ALU.mult)
    ts(sb("U2"), sb("XI", 0, 128), col(0), ALU.is_lt, -1.0, ALU.mult)
    tt(sb("NU"), sb("U1"), sb("U2"), ALU.mult)
    ts(sb("K16"), sb("XI", 0, 16), col(1), ALU.is_equal)
    ts(sb("JT", 0, 32), sb("XI", 0, 32), 16.0, ALU.mult, col(1), ALU.add)
    for t in range(1, TR):
        ts(sb("JT", 32 * t, 32 * t + 32), sb("JT", 0, 32), float(RO * t), ALU.add)
    cp(sb("OF"), sb("JT", 0, 32))
    ts(sb("V384"), sb("JT", 0, 24), float(SO), ALU.add)
    fill(sb("KC", 0, 24), 576.0)
    fill(sb("KC", 24, 48), 64.0)
    fill(sb("MK"), 1.0)
    fill(sb("MK", 0, 1024, 16), 0.0)
    fill(sb("SC", 0, 8), 0.0)
    fill(sb("DD", 0, 8), 0.0)
    fill(sb("CP"), 0)
    sel = lambda i: sb("ZZ", 15 - i, 143 - i)

    load_slots("CT", 0, "rCD", [0])
    load_slots("TE", SO, "rED", [0])
    dma([(sb("AB", 0, 32), dr("rABD", 0, N, 0, 64)), (sb("AB", 32, 64), dr("rABD", 0, N, 64, 128))], 256, 128)
    if C0_PE < N - 1:
        load_slots("CT", 0, "rCD", list(range(1, N - C0_PE)))
    for d in range(N - C0_PE, N):
        b = bank()
        mm([(ps(b, 0, SO), sb("I2", 16 * d, 16 * d + 128), sb("CT", 0, SO), True, True)], True)
        cp(sb("CT", SO * d, SO * d + SO), ps(b, 0, SO), "VS")
    dma([(sb("KK"), dr("rKD", 0, N))], 128, 4 * RO)
    dma([(sb("PK"), dr("rPD", 0, N))], 128, 4 * SO)
    dma([(sb("TE", 0, SO), dr("rTD", 0, N))], 128, 4 * SO)
    ts(sb("A1"), sb("AB"), col(4), ALU.subtract)
    ts(sb("A2"), sb("A1"), 0.0, ALU.is_lt, float(N * SO), ALU.mult)
    tt(sb("A3"), sb("A1"), sb("A2"), ALU.add)
    cp(sb("OA"), sb("A3"))
    ts(sb("A4"), sb("A3"), 4, ALU.arith_shift_right)
    cp(sb("CA"), sb("A4"))
    ts(sb("A5"), sb("A3"), 15, ALU.bitwise_and)
    cp(sb("AM"), sb("A5"))

    def flags(ranges):
        for (c0, c1) in ranges:
            ts(sb("FL", c0, c1), sb("TE", SO + c0, SO + c1), 0.125, ALU.is_ge)

    def counts(t):
        mm([(ps(0, 0, 24), sel(i), sb("FL", i, SO, 16), i == 0, i == 15) for i in range(16)], False)
        cp(sb("CN", 24 * t, 24 * t + 24), ps(0, 0, 24))
        pass_counts(t)
        ts(sb("TH"), sb("CN", 24 * t, 24 * t + 24), -2.0, ALU.mult, 24.0, ALU.add)

    def rates(t):
        tt(sb("T1"), ind(sb("CT"), sb("OA", 0, 32)), sb("KK"), ALU.mult)
        tt(sb("WC", RO * t, RO * t + RO), ind(sb("CT"), sb("OA", 32, 64)), sb("T1"), ALU.mult)

    flags([(0, SO)])
    counts(0)
    if E0_PE < N - 1:
        load_slots("TE", SO, "rED", list(range(1, N - E0_PE)))
    for d in range(N - E0_PE, N):
        b = bank()
        mm([(ps(b, 0, SO), sb("I2", 16 * d, 16 * d + 128), sb("TE", SO, 2 * SO), True, True)], True)
        cp(sb("TE", SO + SO * d, 2 * SO + SO * d), ps(b, 0, SO), "VS")
    rates(0)
    cp(sb("MA"), ind(sb("K16"), sb("AM")), "VS")

    ch = lambda nm, k, o=0: sb(nm, o + 1024 * k, o + 1024 * k + 1024)

    def unpack(lo, lr, both, tmp):
        ts(tmp, both, N * RO - 1, ALU.bitwise_and)
        cp(lo, tmp)
        ts(lr, both, 1.0 / (N * RO), ALU.mult, -0.375, ALU.add)
    unpack(sb("LOA"), sb("LRA"), sb("PK"), sb("OT2"))

    for t in range(TR):
        last = t == TR - 1
        part[0], part[1] = "a", t
        nb = sb("NB", 24 * t, 24 * t + 24)
        tt(sb("LF", 0, 24), nb, sb("TH"), ALU.is_ge)
        tt(sb("LF", 24, 48), nb, sb("TH"), ALU.is_lt)
        lv, fz = sb("LF", 0, 24), sb("LF", 24, 48)
        if t:
            mm([(ps(1, 24 * d, 24 * d + 24), sb("IB", 16 * d, 16 * d + 128), lv, True, True) for d in range(N)], False)
            cp(sb("L2"), ps(1, 0, 192), "VS")
            for h in (0, 1):
                got, mask = ind(sb("L2"), sb("CA", 32 * h, 32 * h + 32)), sb("MA", RO * h, RO * h + RO)
                if h + GG_S >= 2:
                    b = bank()
                    mm([(ps(b, 0, RO), sb("IB", 0, 128), mask, True, True)], False)
                    cp(sb("GB", RO * h, RO * h + RO), got, "S")
                    got, mask = sb("GB", RO * h, RO * h + RO), ps(b, 0, RO)
                tt(sb("GG", RO * h, RO * h + RO), got, mask, ALU.mult)
                mm([(ps(1, 256, 288), sel(i), sb("GG", RO * h + i, RO * h + RO, 16), h == 0 and i == 0, h == 1 and i == 15)
                    for i in range(16)], False)
        count_up("F1", "LF", 24, 6 * t, 24.0)
        mm([(ps(0, 32, 56), sb("BD"), sb("F1"), True, False), (ps(0, 32, 56), sb("NU"), lv, False, True),
            (ps(0, 56, 80), sb("BD"), sb("FF", 24 - 6 * t, 48 - 6 * t), True, False), (ps(0, 56, 80), sb("NBD"), sb("F1"), False, False),
            (ps(0, 56, 80), sb("NU"), fz, False, True)], False)
        tt(sb("YY"), ps(0, 32, 80), sb("KC"), ALU.min)
        tt(sb("OO"), ps(0, 32, 80), sb("KC"), ALU.is_le)
        tt(sb("PL"), sb("OO"), sb("LF"), ALU.mult)
        tt(sb("PS1"), sb("YY", 0, 24), sb("YY", 24, 48), ALU.add)
        tt(sb("PKD"), sb("PL", 0, 24), sb("PL", 24, 48), ALU.add)
        tt(sb("TT"), sb("PS1"), sb("PKD"), ALU.mult)
        tt(sb("SF"), sb("TT"), sb("JT", 0, 24), ALU.max)
        cp(sb("SCO"), sb("SF"))
        for (c0, c1) in ((96 * t + 64, SO), (0, 96 * t)):
            if c0 < c1:
                cp(ind(sb("CP"), sb("SCO", c0 // 16, c1 // 16)), sb("PK", c0, c1))
        unpack(sb("LO", 64, 256), sb("LR", 64, 256), sb("CP", 449, 641), sb("LI", 0, 192))
        lst = lambda nm, k: sb(nm, 64 * k, 64 * k + 64) if k else sb(nm + "A", 96 * t, 96 * t + 64)
        ts(sb("BK"), sb("TT"), 16.0, ALU.mult, -6137.0, ALU.add)
        tt(sb("TL"), sb("PS1"), sb("PL", 0, 24), ALU.mult)
        ts(sb("BC"), sb("TL"), -377.0, ALU.add)
        ts(sb("Q1"), sb("PKD"), -float(SO), ALU.mult)
        tt(sb("Q2"), sb("Q1"), sb("V384"), ALU.add)
        cp(sb("TQ"), sb("Q2"))
        cp(sb("T2"), ind(sb("TE", 0, 2 * SO), sb("TQ")), "VS")
        if t:
            ts(sb("G1"), ps(1, 256, 288), 0.0, ALU.is_gt)
            count_up("G2", "G1", 32, 8 * t, 0.0)
            tt(sb("FJ"), sb("G1"), sb("JT", 32 * t, 32 * t + 32), ALU.mult)
            mm([(ps(0, 96, 128), sb("BD"), sb("G2"), True, False), (ps(0, 96, 128), sb("NU"), sb("G1"), False, True)], False)
            ts(sb("M2"), ps(0, 96, 128), 256.0, ALU.is_le)
            tt(sb("O2"), sb("M2"), sb("FJ"), ALU.mult)
            tt(sb("OF"), sb("OF"), sb("O2"), ALU.max)
            cp(sb("OW"), sb("OF"))
            now = ind(sb("WC", 0, RO * t + RO), sb("OW"))
        else:
            now = sb("WC", 0, RO)
        ts(sb("WM", 0, RO), now, 1.0, ALU.min)
        spread("WM", 0, RO, [(0, RO)], W_PE)
        cp(sb("W8", 0, RO), now, "S", 0.125)
        spread("W8", 0, RO, [(0, RO)], W8_PE)
        if last:
            cp(sb("YW"), now, "VS")
            go_home("OWD", "YW", 0, [(0, RO)], "yw")

        blocks = [(96 * ((t + k) % 4), 96 * ((t + k) % 4) + 96) for k in range(4)]
        join = lambda a, b: [(a[0], b[1])] if a[1] == b[0] else [a, b]
        head, tail = join(blocks[0], blocks[1]), join(blocks[2], blocks[3])

        def finish(ranges, done):
            for (c0, c1) in ranges:
                tt(sb("TE", SO + c0, SO + c1), ind(sb("SC", 0, 8 + 1024 * done), sb("BK", c0 // 16, c1 // 16)), sb("T2", c0, c1), ALU.max)

        def tree(k0, m):
            for h in range(m):
                x = 1024 * (k0 + h)
                b = 2 if k0 + h == 3 else 6
                mm([(ps(b, 0, 512), sb("I2", 0, 128), sb("RW", x + 1, x + 1024, 2), True, True)], True)
                tt(sb("YE", 256 * h, 256 * h + 256), sb("RW", x, x + 1024, 4), ps(b, 0, 512, 2), ALU.add)
                tt(ps(7, 256 * h, 256 * h + 256), sb("RW", x + 2, x + 1024, 4), ps(b, 1, 512, 2), ALU.add)
            tt(sb("ZE", 0, 128 * m), sb("YE", 0, 256 * m, 2), ps(7, 0, 256 * m, 2), ALU.add)
            tt(ps(6, 0, 128 * m), sb("YE", 1, 256 * m, 2), ps(7, 1, 256 * m, 2), ALU.add)
            tt(sb("PP", 0, 64 * m), sb("ZE", 0, 128 * m, 2), ps(6, 0, 128 * m, 2), ALU.add)
            tt(ps(7, 0, 64 * m), sb("ZE", 1, 128 * m, 2), ps(6, 1, 128 * m, 2), ALU.add)
            tt(sb("DD", 8 + 64 * k0, 8 + 64 * (k0 + m)), sb("PP", 0, 64 * m), ps(7, 0, 64 * m), ALU.subtract)

        def amounts(ranges, done, npe):
            for (c0, c1) in ranges:
                tt(sb("CX", c0, c1), ind(sb("DD", 0, 8 + 64 * done), sb("BC", c0 // 16, c1 // 16)), sb("CT", c0, c1), ALU.add)
                ts(sb("CT", c0, c1), sb("CX", c0, c1), 0.125, ALU.max, 8.0, ALU.min)
            if not last:
                spread("CT", 0, SO, ranges, npe)

        for sweep in (0, 1):
            nd = NDIRECT[sweep]
            part[0] = "bc"[sweep]
            early, late = (("EG", "MW"), ("MW", "EG"))[sweep]
            for k in range(4):
                if nd[k] != "E":
                    cp(ch("EG", k), ind(ETAB, lst("LO", k)), "S" if sweep else "VS")
            if sweep == 0:
                for k in range(4):
                    cp(ch("MW", k), ind(sb("WM"), lst("LR", k)), "S")
                for k in range(4):
                    cp(ch("RW", k), ind(sb("W8"), lst("LR", k)), "S")
            for k in range(4):
                if nd[k] == "W":
                    tt(ch("PR", k), ind(sb("WM"), lst("LR", k)), ch("EG", k), ALU.mult)
                elif nd[k] == "E":
                    tt(ch("PR", k), ind(ETAB, lst("LO", k)), ch("MW", k), ALU.mult)
                else:
                    b = 2 + 2 * (k % 2)
                    for h in (0, 1):
                        x = 1024 * k + 512 * h
                        mm([(ps(b + h, 0, 512), sb("I2", 0, 128), sb(early, x, x + 512), True, True)], True)
                    tt(ch("PR", k), ch(late, k), ps(b, 0, 1024), ALU.mult)
                scan(ch("SC", k, 8), sb("MK"), ch("PR", k), 0.0, ALU.mult, ALU.max)
                if k == 2:
                    part[0] = "hj"[sweep]
                    finish(head, 3)
                    if last and sweep:
                        go_home("OH", "TE", SO, head, "ye")
                    else:
                        spread("TE", SO, SO, head, HEAD_PE[sweep] + (3 if len(head) > 1 else 0))
                        if sweep:
                            flags(head)
            part[0] = "tu"[sweep]
            finish(tail, 4)
            if last and sweep:
                go_home("OE", "TE", SO, tail, "ye")
            else:
                if sweep:
                    flags(tail)
                    counts(t + 1)
                spread("TE", SO, SO, tail, TAIL_PE[sweep])
            if sweep == 0:
                part[0] = "d"
                tree(0, 2)
                if C_SPLIT and not last:
                    part[0] = "g"
                    tree(2, 1)
                    amounts(head, 3, 0)
        part[0] = "e"
        if C_SPLIT and not last:
            tree(3, 1)
            part[0] = "f"
            amounts(tail, 4, C_PE)
        else:
            tree(2, 2)
            part[0] = "f"
            amounts([(0, SO)], 4, C_PE)
        if last:
            go_home("OC", "CT", 0, [(0, SO)], "yc")
        else:
            rates(t + 1)
    return ops, cnt, Q


def order(ops):
    n = len(ops)
    pred = [list(o["deps"].items()) for o in ops]
    succ = [[] for o in ops]
    for i in range(n):
        for d, kind in pred[i]:
            succ[d].append((i, kind))

    def gap(p, ep, e, kind):
        return 0.0 if kind == "order" or (ep == e and (e == "P" or kind == "bank")) else ops[p]["lat"] + HOP

    def place(key, on, back):
        first, then = (succ, pred) if back else (pred, succ)
        left = [len(x) for x in first]
        ready = [i for i in range(n) if not left[i]]
        start, end, seq, busy, on = [0.0] * n, [0.0] * n, [0] * n, {e: [] for e in "VSPGYR"}, list(on)
        for step in range(n):
            i = min(ready, key=lambda x: key[x])
            ready.remove(i)
            best = None
            for e in (on[i] if back else ops[i]["eng"]):
                t0 = ops[i]["lat"] if back else 0.0
                for d, kind in first[i]:
                    t0 = max(t0, end[d] + (gap(i, e, on[d], kind) if back else gap(d, on[d], e, kind)))
                dur, at, iv = ops[i]["dur"][e], 0, busy[e]
                if e != "R":
                    at = len(iv)
                    while at and iv[at - 1][1] > t0:
                        at -= 1
                    while at < len(iv) and t0 + dur > iv[at][0]:
                        t0 = max(t0, iv[at][1])
                        at += 1
                cost = t0 + dur + (VCOST * dur if e == "V" else 0.0)
                if best is None or cost < best[0] - 1e-9:
                    best = (cost, t0, e, at, t0 + dur)
            start[i], on[i], end[i], seq[i] = best[1], best[2], best[4], step
            if best[2] != "R":
                busy[best[2]].insert(best[3], (best[1], best[4]))
            for s, kind in then[i]:
                left[s] -= 1
                if not left[s]:
                    ready.append(s)
        return start, end, on, seq, max(end[i] + ops[i]["lat"] for i in range(n))

    rng = np.random.RandomState(SEED)
    level = [0.0] * n
    for i in range(n - 1, -1, -1):
        level[i] += min(ops[i]["dur"].values()) + ops[i]["lat"] + HOP
        for d, kind in pred[i]:
            level[d] = max(level[d], level[i])
    if SHIFT:
        key, best = [SHIFT[o["tag"]] + PERIOD * o["round"] + 1e-6 * i for i, o in enumerate(ops)], None
    else:
        key, best = [BIAS.get(ops[i]["tag"], 0.0) - level[i] for i in range(n)], None
    for k in range(PASSES + 1):
        noise = rng.uniform(-NOISE, NOISE, n) if SEED else np.zeros(n)
        got = place([key[i] + float(noise[i]) for i in range(n)], [None] * n, False)
        if best is None or got[4] < best[4]:
            best = got
        if k < PASSES:
            rev = place([-x for x in got[1]], got[2], True)
            key = [-x for x in rev[1]]
    return sorted(range(n), key=lambda x: (best[0][x], best[3][x])), best[2]


def rank_program(g, core, T, topo):
    if T.rank_of(core) is None:
        return
    ops, cnt, Q = build(g, core, T, topo, PACE[0])
    if "seq" not in PLAN:
        code = [62 * DIGITS.index(ORDER[k]) + DIGITS.index(ORDER[k + 1]) for k in range(0, len(ORDER), 2)]
        PLAN["seq"], PLAN["on"] = [x // 2 for x in code], [o["eng"][0] for o in ops]
        for x in code:
            if x % 2:
                PLAN["on"][x // 2] = "S"
        if not ORDER:
            PLAN["seq"], PLAN["on"] = order(ops)
    seq = PLAN["seq"]
    place = {i: k for k, i in enumerate(seq)}
    assert len(seq) == len(ops) and all(place[d] < place[i] for i in seq for d in ops[i]["deps"])
    for i, o in enumerate(ops):
        o["start"], o["on"] = place[i], PLAN["on"][i]

    def needs(o):
        return [d for d, kind in o["deps"].items()
                if kind != "order" and not (ops[d]["on"] == o["on"] and (o["on"] == "P" or kind == "bank"))]

    pos, know, waits = {}, {e: {} for e in "VSPGY"}, {}
    for i in seq:
        o = ops[i]
        if o["kind"] == "c":
            pos[o["on"]] = pos.get(o["on"], 0) + 1
            o["key"] = ("q" + o["on"], pos[o["on"]])
        elif o["kind"] == "d":
            o["key"] = (o["sem"], 1)
        elif o["kind"] == "a":
            o["key"] = (o["tok"][0], 1)
            o["clock"] = {o["tok"][0]: 1}
            continue
        k, w = know[o["on"]], []
        for d in sorted(needs(o), key=lambda x: -ops[x]["start"]):
            s, v = ops[d]["key"]
            if k.get(s, 0) < v:
                w.append(d)
                ops[d]["signal"] = True
                for s2, v2 in ops[d]["clock"].items():
                    k[s2] = max(k.get(s2, 0), v2)
        waits[i] = w
        if o["kind"] != "r":
            o["clock"] = dict(k)
            o["clock"][o["key"][0]] = o["key"][1]
    total, seen = {}, {}
    for i in seq:
        o = ops[i]
        if o["kind"] == "a":
            total[o["tok"][0]] = o["tok"][1]
            continue
        for d in waits[i]:
            s, v = ops[d]["tok"]
            Q[o["on"]].wait_ge(T.sem[s], v)
            seen[s] = max(seen.get(s, 0), v)
        ins = o["fn"](o["on"])
        if o["kind"] == "d" or o.get("signal"):
            s, step = o["key"][0], 16 if o["kind"] == "d" else 1
            for x in ins:
                x.then_inc(T.sem[s], step)
                total[s] = total.get(s, 0) + step
            o["tok"] = (s, total[s])
    total["left"] = cnt["left"]
    for s in total:
        if seen.get(s, 0) < total[s]:
            g.wait_ge(T.sem[s], total[s])
